import numpy as np
import ml_dtypes


def mxq(x, axis, fmt="e4m3"):
    dtype, down = {"e4m3": (ml_dtypes.float8_e4m3fn, 7), "e5m2": (ml_dtypes.float8_e5m2, 14)}[fmt]
    v = np.moveaxis(np.asarray(x, np.float32).astype(ml_dtypes.bfloat16).astype(np.float64), axis, -1)
    blocks = v.reshape(v.shape[:-1] + (-1, 32))
    amax = np.abs(blocks).max(-1, keepdims=True)
    byte = np.maximum(np.where(amax > 0, np.frexp(amax)[1] - 1 + 127, 0) - down, 1)
    scale = np.exp2(byte - 127.0)
    codes = (blocks / scale).astype(np.float32).astype(dtype).astype(np.float64)
    return np.moveaxis((codes * scale).reshape(v.shape), -1, axis)


WIDE = False


def mx_kscale(k):
    if not WIDE:
        return np.ones(k)
    levels = np.array([10, -10, 5, -5, 0])
    if k % 512:
        return np.exp2(np.random.permutation(np.resize(levels, k // 32))).repeat(32)
    a = np.empty((k // 512, 16))
    for p in range(k // 512):
        a[p, :8] = np.random.permutation(np.resize(levels, 8))
        for g in range(8):
            far = levels[np.abs(levels - a[p, g]) >= 10]
            a[p, g + 8] = far[np.random.randint(len(far))]
    return np.exp2(a.ravel()).repeat(32)


def f64(x):
    return np.asarray(x).astype(np.float64)


def striped(idx):
    return np.tile(idx.reshape(-1, 16).T, (8, 1)).astype(np.uint16)


def unstriped(offs):
    return offs[:16].T.reshape(-1).astype(np.int64)


E2M1 = np.array([0.0, 0.5, 1.0, 1.5, 2.0, 3.0, 4.0, 6.0, -0.0, -0.5, -1.0, -1.5, -2.0, -3.0, -4.0, -6.0])


def pack_weight(w, fmt):
    k, n = w.shape
    w = f64(np.asarray(w, np.float32).astype(ml_dtypes.bfloat16)).reshape(k // 32, 32, n)
    amax = np.abs(w).max(1)
    if fmt == "e4m3":
        byte = np.frexp(amax)[1] - 1 + 127 - 7
    else:
        mant, ex = np.frexp(amax / 6.0)
        byte = np.where(mant > 0.5, ex, ex - 1) + 127
    byte = np.clip(np.where(amax > 0, byte, 1), 1, 254)
    scaled = (w * np.exp2(127.0 - byte)[:, None, :]).reshape(k, n).astype(np.float32)
    by_word = np.ascontiguousarray(scaled.reshape(k // 512, 128, 4, n).transpose(0, 1, 3, 2))
    if fmt == "e4m3":
        words = by_word.astype(ml_dtypes.float8_e4m3fn).view(np.uint8)
    else:
        c = by_word.astype(ml_dtypes.float4_e2m1fn).view(np.uint8) & 0xF
        words = (c[..., 0::2] | (c[..., 1::2] << 4)).reshape(k // 512, 128, 2 * n)
    return np.ascontiguousarray(words), np.ascontiguousarray(byte.astype(np.uint8).reshape(k // 512, 16, n))


def unpack_weight(words, scales, fmt):
    g, _, n = scales.shape
    words = np.ascontiguousarray(words).reshape(g, 128, n, -1)
    if fmt == "e4m3":
        vals = words.view(ml_dtypes.float8_e4m3fn).astype(np.float64)
    else:
        nib = np.empty((g, 128, n, 4), np.uint8)
        nib[..., 0::2] = words & 0xF
        nib[..., 1::2] = words >> 4
        vals = E2M1[nib]
    vals = vals * np.repeat(np.exp2(scales.astype(np.float64) - 127.0), 8, axis=1)[..., None]
    return vals.transpose(0, 1, 3, 2).reshape(g * 512, n)


def gelu(v):
    return 0.5 * v * (1.0 + np.tanh(np.sqrt(2.0 / np.pi) * (v + 0.044715 * v**3)))


def bf(x):
    return np.asarray(x, np.float32).astype(ml_dtypes.bfloat16)


def planes(Y):
    n, m = Y.shape
    b = f64(bf(Y)).reshape(n // 32, 32, m)
    amax = np.abs(b).max(1)
    byte = np.clip(np.where(amax > 0, np.frexp(amax)[1] - 1 + 127 - 7, 1), 1, 254)
    codes = (b * np.exp2(127.0 - byte)[:, None, :]).reshape(n, m).astype(np.float32).astype(ml_dtypes.float8_e4m3fn).view(np.uint8)
    words = codes.reshape(n // 512, 128, 4, m).transpose(0, 1, 3, 2)
    return np.ascontiguousarray(words), np.ascontiguousarray(byte.astype(np.uint8).reshape(n // 512, 16, m))


T, S, P, K, H, N = 4096, 1024, 512, 1024, 1536, 512


def setup_inputs():
    n = np.random.standard_normal
    s = mx_kscale(K)[:, None]
    u = mx_kscale(H)[:, None]
    size = np.exp(0.8 * n(N))
    d = {}
    d["tab_words"], d["tab_scales"] = pack_weight(n((K, T)) * s, "e4m3")
    d["offs"] = striped(np.random.permutation(T)[:S])
    d["w1"] = (2.0 * n((K, H)) / K ** 0.5 / s).astype(np.float32)
    d["gain"] = (np.exp(0.3 * n(H)) * u[:, 0]).astype(np.float32)
    d["w2_words"], d["w2_scales"] = pack_weight(0.5 * n((H, N)) / H ** 0.5 / u * size, "e2m1")
    d["rest"] = (size * n(N)).astype(np.float32)
    d["ratio"] = np.exp(0.4 * n(N)).astype(np.float32)
    d["pos1"] = striped(np.random.permutation(S)[:P])
    d["pos2"] = striped(np.random.permutation(S)[:P])
    return d


def reference(tab_words, tab_scales, offs, w1, gain, w2_words, w2_scales, rest, ratio, pos1, pos2):
    v = unpack_weight(tab_words, tab_scales, "e4m3")[:, unstriped(offs)]
    sway = mxq(f64(w1), 0, "e4m3").T @ v
    h = np.sqrt(np.square(sway) + 1.0) * f64(gain)[:, None]
    w2 = unpack_weight(w2_words, w2_scales, "e2m1")
    g2 = (w2.T @ mxq(h, 0, "e4m3")) - f64(rest)[:, None]
    jib = g2[:, unstriped(pos1)]
    hook = g2[:, unstriped(pos2)]
    y = np.maximum(jib, f64(ratio)[:, None] * hook)
    words, scales = planes(y)
    return y, words, scales

@@ -1,0 +1,280 @@
+from contextlib import ExitStack
+
+import concourse.mybir as mybir
+
+T, S, PAIRS, K, H, N = 4096, 1024, 512, 1024, 1536, 512
+FLOPS = 2 * K * H * S + 2 * H * N * S
+
+F32 = mybir.dt.float32
+BF16 = mybir.dt.bfloat16
+I32 = mybir.dt.int32
+U32 = mybir.dt.uint32
+U16 = mybir.dt.uint16
+U8 = mybir.dt.uint8
+E4M3 = mybir.dt.float8_e4m3fn_x4
+E2M1 = mybir.dt.float4_e2m1fn_x4
+ACT = mybir.ActivationFunctionType
+ALU = mybir.AluOpType
+
+P = 128
+PACK = 4
+PASS = P * PACK
+K_PASSES = K // PASS
+R_PASSES = H // PASS
+HALF = S // 2
+CHUNK = 128
+
+
+def tile_list_slew_sway_features_kernel(
+    tc, tab_words, tab_scales, offs, w1, gain, w2_words, w2_scales, rest, ratio, pos1, pos2, out_0, out_1, out_2
+):
+    nc = tc.nc
+    with ExitStack() as ctx:
+        keep = ctx.enter_context(tc.tile_pool(name="keep", bufs=1))
+        ring = ctx.enter_context(tc.tile_pool(name="ring", bufs=3))
+        psum = ctx.enter_context(tc.psum_pool(name="psum", bufs=4))
+
+        offs_t = keep.tile([P, S // 16], U16, name="offs_t")
+        nc.sync.dma_start(offs_t[:], offs)
+
+        tab_s = keep.tile([P, K_PASSES, T], U8, name="tab_s", align_bytes=64)
+        nc.vector.memset(tab_s[:].bitcast(I32), 0)
+        w2_s_raw = keep.tile([P, R_PASSES, N], U8, name="w2_s_raw", align_bytes=64)
+        nc.gpsimd.memset(w2_s_raw[:].bitcast(I32), 0)
+        one_in = keep.tile([P, 1], F32, name="one_in")
+        nc.gpsimd.memset(one_in[:], 1.0)
+        one = keep.tile([P, 1], F32, name="one")
+        nc.scalar.activation(one[:], one_in[:], ACT.Sqrt)
+
+        tab_w = [keep.tile([P, T], I32, name="tab_w%d" % a, align_bytes=64) for a in range(K_PASSES)]
+
+        def load_tab(a):
+            nc.sync.dma_start(tab_w[a][:], tab_words[a].rearrange("p t i -> p (t i)").bitcast(I32))
+
+        def load_w1(b, a, c0, width, tag, bufs):
+            raw = ring.tile([P, PACK, width], F32, name=tag, tag=tag, bufs=bufs)
+            rows = w1[a * PASS : (a + 1) * PASS, b * PASS + c0 : b * PASS + c0 + width]
+            nc.sync.dma_start(raw[:], rows.rearrange("(p j) c -> p j c", j=PACK))
+            return raw
+
+        load_tab(0)
+        for q in range(4):
+            nc.sync.dma_start(
+                tab_s[32 * q : 32 * q + 4, :, :].bitcast(I32),
+                tab_scales[:, 4 * q : 4 * q + 4, :].rearrange("a r c -> r a c").bitcast(I32),
+            )
+        w2_raw = keep.tile([P, R_PASSES, 2 * N], U8, name="w2_raw", align_bytes=64)
+        nc.sync.dma_start(w2_raw[:].bitcast(I32), w2_words.rearrange("a p c -> p a c").bitcast(I32))
+        raw00 = load_w1(0, 0, 0, PASS, "raw", 3)
+        for q in range(4):
+            nc.sync.dma_start(
+                w2_s_raw[32 * q : 32 * q + 4, :, :].bitcast(I32),
+                w2_scales[:, 4 * q : 4 * q + 4, :].rearrange("a r c -> r a c").bitcast(I32),
+            )
+        load_tab(1)
+        raw01 = [load_w1(0, 1, i * PASS // 2, PASS // 2, "raw_half%d" % i, 1) for i in range(2)]
+        gain_t = keep.tile([P, R_PASSES, PACK], F32, name="gain_t")
+        nc.sync.dma_start(gain_t[:], gain.rearrange("(b p t) -> p b t", p=P, t=PACK))
+
+        v_w = {}
+
+        def gather_words(a, h):
+            v_w[a, h] = keep.tile([P, HALF], U32, name="v_w%d%d" % (a, h), align_bytes=64)
+            cols = slice(h * HALF // 16, (h + 1) * HALF // 16)
+            nc.vector.tensor_copy(v_w[a, h][:], tab_w[a][:].bitcast(U32).indirect(offs_t[:, cols]))
+
+        w1_w, w1_s = {}, {}
+
+        def round_w1(grouped, raw, m0, m1, engine):
+            dst = grouped[:].rearrange("p (t m j) -> p m j t", t=PACK, j=PACK)[:, m0:m1, :, :]
+            src = raw[:].rearrange("p j (m t) -> p m j t", t=PACK)
+            if engine == "scalar":
+                nc.scalar.copy(dst, src)
+            else:
+                nc.vector.tensor_copy(dst, src)
+
+        def quantize_w1(b, a, grouped):
+            w1_w[b, a] = keep.tile([P, PASS], U32, name="w1_w%d%d" % (b, a), align_bytes=64)
+            w1_s[b, a] = keep.tile([P, PASS], U8, name="w1_s%d%d" % (b, a), align_bytes=64)
+            nc.vector.quantize_mx(w1_w[b, a][:].bitcast(E4M3), w1_s[b, a][:], grouped[:])
+
+        def new_grouped():
+            return ring.tile([P, PACK * PASS], BF16, name="grouped", align_bytes=64)
+
+        gather_words(0, 0)
+        gather_words(0, 1)
+        g00 = new_grouped()
+        round_w1(g00, raw00, 0, P, "scalar")
+        v_s = [keep.tile([P, S], U8, name="v_s%d" % a, align_bytes=64) for a in range(K_PASSES)]
+        for a in range(K_PASSES):
+            nc.vector.tensor_copy(v_s[a][:], tab_s[:, a, :].indirect(offs_t[:]))
+        w2_w = keep.tile([P, R_PASSES, 2 * N], U8, name="w2_w", align_bytes=64)
+        nc.vector.tensor_copy(
+            w2_w[:].bitcast(U16).rearrange("p a (t q) -> p a q t", t=PACK),
+            w2_raw[:].bitcast(U16).rearrange("p a (q t) -> p a q t", t=PACK),
+        )
+        w2_s = keep.tile([P, R_PASSES, N], U8, name="w2_s", align_bytes=64)
+        nc.vector.tensor_copy(
+            w2_s[:].rearrange("p a (t q) -> p a q t", t=PACK),
+            w2_s_raw[:].rearrange("p a (q t) -> p a q t", t=PACK),
+        )
+
+        quantize_w1(0, 0, g00)
+        gather_words(1, 0)
+        g01 = new_grouped()
+        round_w1(g01, raw01[0], 0, P // 2, "scalar")
+        gather_words(1, 1)
+        round_w1(g01, raw01[1], P // 2, P, "vector")
+        quantize_w1(0, 1, g01)
+
+        later = [(b, a) for b in range(1, R_PASSES) for a in range(K_PASSES)]
+        raws = {ba: load_w1(ba[0], ba[1], 0, PASS, "raw", 3) for ba in later}
+        pos1_t = keep.tile([P, PAIRS // 16], U16, name="pos1_t")
+        nc.sync.dma_start(pos1_t[:], pos1)
+        pos2_t = keep.tile([P, PAIRS // 16], U16, name="pos2_t")
+        nc.sync.dma_start(pos2_t[:], pos2)
+        rest_t = keep.tile([P, PACK], F32, name="rest_t")
+        nc.sync.dma_start(rest_t[:], rest.rearrange("(p t) -> p t", t=PACK))
+        ratio_t = keep.tile([P, PACK], F32, name="ratio_t")
+        nc.sync.dma_start(ratio_t[:], ratio.rearrange("(p t) -> p t", t=PACK))
+        neg_rest = keep.tile([P, PACK], F32, name="neg_rest")
+        nc.gpsimd.tensor_scalar(neg_rest[:], rest_t[:], -1.0, 0.0, ALU.mult, ALU.add)
+
+        h_w = {(b, h): keep.tile([P, HALF], U32, name="h_w%d%d" % (b, h), align_bytes=64) for b in range(R_PASSES) for h in range(2)}
+        h_s = {(b, h): keep.tile([P, HALF], U8, name="h_s%d%d" % (b, h), align_bytes=64) for b in range(R_PASSES) for h in range(2)}
+        g2 = [keep.tile([P, S], F32, name="g2_%d" % t) for t in range(PACK)]
+
+        steps = []
+        for b, h in ((0, 0), (0, 1), (1, 0), (2, 0), (1, 1), (2, 1)):
+            steps.append((b, h, 0, 2 * CHUNK))
+            if (b, h) == (2, 1):
+                steps.append((b, h, 2 * CHUNK, CHUNK))
+                steps.append((b, h, 3 * CHUNK, CHUNK))
+            else:
+                steps.append((b, h, 2 * CHUNK, 2 * CHUNK))
+
+        squares, roots, rounded = {}, {}, {}
+
+        def square(i):
+            b, h, c0, width = steps[i]
+            squares[i] = ring.tile([P, width, PACK], F32, name="sq")
+            for c in range(0, width, CHUNK):
+                bank = psum.tile([P, PACK, CHUNK], F32, name="sway")
+                cols = slice(c0 + c, c0 + c + CHUNK)
+                scols = slice(h * HALF + c0 + c, h * HALF + c0 + c + CHUNK)
+                for t in range(PACK):
+                    tc_ = slice(t * P, (t + 1) * P)
+                    for a in range(K_PASSES):
+                        nc.tensor.matmul_mx(
+                            bank[:, t, :],
+                            lhsT=w1_w[b, a][:, tc_].bitcast(E4M3),
+                            lhsT_scale=w1_s[b, a][:, tc_],
+                            rhs=v_w[a, h][:, cols].bitcast(E4M3),
+                            rhs_scale=v_s[a][:, scols],
+                            start=(a == 0),
+                            stop=(a == K_PASSES - 1),
+                        )
+                nc.scalar.activation(squares[i][:, c : c + CHUNK, :], bank[:].rearrange("p t n -> p n t"), ACT.Square)
+
+        def root(i):
+            width = steps[i][3]
+            roots[i] = ring.tile([P, width, PACK], F32, name="root")
+            nc.scalar.activation(roots[i][:], squares[i][:], ACT.Sqrt, bias=one[:])
+
+        def apply_gain(i):
+            b, h, c0, width = steps[i]
+            rounded[i] = ring.tile([P, width, PACK], BF16, name="h_bf", align_bytes=64)
+            nc.vector.tensor_tensor(
+                rounded[i][:], roots[i][:], gain_t[:, b : b + 1, :].broadcast_to([P, width, PACK]), ALU.mult
+            )
+
+        def quantize_h(i):
+            b, h, c0, width = steps[i]
+            cols = slice(c0, c0 + width)
+            nc.vector.quantize_mx(
+                h_w[b, h][:, cols].bitcast(E4M3), h_s[b, h][:, cols], rounded[i][:].rearrange("p n t -> p (n t)")
+            )
+
+        banks = {}
+
+        def second(b, h, c0, width, last):
+            cols = slice(c0, c0 + width)
+            for t in range(PACK):
+                if b == 0:
+                    banks[h, t] = psum.tile([P, HALF], F32, name="feat")
+                nc.tensor.matmul_mx(
+                    banks[h, t][:, cols],
+                    lhsT=w2_w[:, b, 2 * t * P : 2 * (t + 1) * P].bitcast(E2M1),
+                    lhsT_scale=w2_s[:, b, t * P : (t + 1) * P],
+                    rhs=h_w[b, h][:, cols].bitcast(E4M3),
+                    rhs_scale=h_s[b, h][:, cols],
+                    start=(b == 0),
+                    stop=last,
+                )
+
+        def after_quantize(i):
+            b, h, c0, width = steps[i]
+            done = c0 + width == HALF
+            if (b, h) == (2, 1):
+                for c in range(c0, c0 + width, CHUNK):
+                    second(b, h, c, CHUNK, c + CHUNK == HALF)
+            elif done and (b, h) != (0, 1):
+                second(b, h, 0, HALF, b == R_PASSES - 1)
+            if done and (b, h) == (2, 0):
+                for t in range(PACK):
+                    nc.scalar.activation(g2[t][:, 0:HALF], banks[0, t][:], ACT.Identity, bias=neg_rest[:, t : t + 1])
+                second(0, 1, 0, HALF, False)
+
+        n_steps = len(steps)
+        for i in range(n_steps + 3):
+            if i < n_steps:
+                square(i)
+            if 1 <= i <= n_steps:
+                root(i - 1)
+            if 2 <= i <= n_steps + 1:
+                apply_gain(i - 2)
+            if 1 <= i <= len(later):
+                b, a = later[i - 1]
+                grouped = new_grouped()
+                round_w1(grouped, raws[b, a], 0, P, "vector")
+            if i >= 3:
+                quantize_h(i - 3)
+                after_quantize(i - 3)
+            if 1 <= i <= len(later):
+                quantize_w1(b, a, grouped)
+
+        for t in range(PACK):
+            nc.scalar.activation(g2[t][:, HALF:S], banks[1, t][:], ACT.Identity, bias=neg_rest[:, t : t + 1])
+
+        y_w = keep.tile([P, PAIRS], U32, name="y_w", align_bytes=64)
+        y_s = keep.tile([P, PAIRS], U8, name="y_s", align_bytes=64)
+        part = PAIRS // 2
+        y_rows = out_0.rearrange("(p t) m -> p t m", t=PACK)
+        words_out = out_1[0].rearrange("p m i -> p (m i)").bitcast(I32)
+        y_bf = []
+        for k in range(2):
+            cols = slice(k * part, (k + 1) * part)
+            lcols = slice(k * part // 16, (k + 1) * part // 16)
+            y = keep.tile([P, PACK, part], F32, name="y%d" % k)
+            for t in range(PACK):
+                jib = ring.tile([P, part], F32, name="jib")
+                nc.vector.tensor_copy(jib[:], g2[t][:].indirect(pos1_t[:, lcols]))
+                hook = ring.tile([P, part], F32, name="hook")
+                nc.vector.tensor_copy(hook[:], g2[t][:].indirect(pos2_t[:, lcols]))
+                if k == 1 and t == 2:
+                    nc.vector.quantize_mx(y_w[:, 0:part].bitcast(E4M3), y_s[:, 0:part], y_bf[0][:])
+                    nc.sync.dma_start(words_out[:, 0:part], y_w[:, 0:part].bitcast(I32))
+                nc.vector.scalar_tensor_tensor(y[:, t, :], hook[:], ratio_t[:, t : t + 1], jib[:], ALU.mult, ALU.max)
+            nc.scalar.dma_start(y_rows[:, :, cols], y[:])
+            y_bf.append(keep.tile([P, PACK * part], BF16, name="y_bf%d" % k, align_bytes=64))
+            dst = y_bf[k][:].rearrange("p (c i t) -> p c t i", i=4, t=PACK)
+            src = y[:].rearrange("p t (c i) -> p c t i", i=4)
+            if k == 0:
+                nc.scalar.copy(dst, src)
+            else:
+                nc.vector.tensor_copy(dst, src)
+        nc.vector.quantize_mx(y_w[:, part:PAIRS].bitcast(E4M3), y_s[:, part:PAIRS], y_bf[1][:])
+        nc.sync.dma_start(words_out[:, part:PAIRS], y_w[:, part:PAIRS].bitcast(I32))
+        for q in range(4):
+            queue = nc.scalar if q % 2 == 0 else nc.sync
+            queue.dma_start(out_2[0, 4 * q : 4 * q + 4, :].bitcast(I32), y_s[32 * q : 32 * q + 4, :].bitcast(I32))

@@ -37,7 +37,7 @@ def tile_list_slew_sway_features_kernel(
         offs_t = keep.tile([P, S // 16], U16, name="offs_t")
         nc.sync.dma_start(offs_t[:], offs)
 
-        tab_s = keep.tile([P, K_PASSES, T], U8, name="tab_s", align_bytes=64)
+        tab_s = keep.tile([P, T], U8, name="tab_s", align_bytes=64)
         nc.vector.memset(tab_s[:].bitcast(I32), 0)
         w2_s_raw = keep.tile([P, R_PASSES, N], U8, name="w2_s_raw", align_bytes=64)
         nc.gpsimd.memset(w2_s_raw[:].bitcast(I32), 0)
@@ -60,8 +60,8 @@ def tile_list_slew_sway_features_kernel(
         load_tab(0)
         for q in range(4):
             nc.sync.dma_start(
-                tab_s[32 * q : 32 * q + 4, :, :].bitcast(I32),
-                tab_scales[:, 4 * q : 4 * q + 4, :].rearrange("a r c -> r a c").bitcast(I32),
+                tab_s[32 * q : 32 * q + 8, :].bitcast(I32),
+                tab_scales[:, 4 * q : 4 * q + 4, :].bitcast(I32),
             )
         w2_raw = keep.tile([P, R_PASSES, 2 * N], U8, name="w2_raw", align_bytes=64)
         nc.sync.dma_start(w2_raw[:].bitcast(I32), w2_words.rearrange("a p c -> p a c").bitcast(I32))
@@ -86,17 +86,21 @@ def tile_list_slew_sway_features_kernel(
         w1_w, w1_s = {}, {}
 
         def round_w1(grouped, raw, m0, m1, engine):
-            dst = grouped[:].rearrange("p (t m j) -> p m j t", t=PACK, j=PACK)[:, m0:m1, :, :]
-            src = raw[:].rearrange("p j (m t) -> p m j t", t=PACK)
+            dst = grouped[:].rearrange("p (u v m j) -> p m u j v", u=2, v=2, j=PACK)[:, m0:m1]
+            src = raw[:].rearrange("p j (m u v) -> p m u j v", u=2, v=2)
             if engine == "scalar":
                 nc.scalar.copy(dst, src)
             else:
                 nc.vector.tensor_copy(dst, src)
 
-        def quantize_w1(b, a, grouped):
+        def quantize_w1(b, a, grouped, pieces=1):
             w1_w[b, a] = keep.tile([P, PASS], U32, name="w1_w%d%d" % (b, a), align_bytes=64)
             w1_s[b, a] = keep.tile([P, PASS], U8, name="w1_s%d%d" % (b, a), align_bytes=64)
-            nc.vector.quantize_mx(w1_w[b, a][:].bitcast(E4M3), w1_s[b, a][:], grouped[:])
+            width = PASS // pieces
+            for c in range(0, PASS, width):
+                nc.vector.quantize_mx(
+                    w1_w[b, a][:, c : c + width].bitcast(E4M3), w1_s[b, a][:, c : c + width], grouped[:, PACK * c : PACK * (c + width)]
+                )
 
         def new_grouped():
             return ring.tile([P, PACK * PASS], BF16, name="grouped", align_bytes=64)
@@ -105,18 +109,17 @@ def tile_list_slew_sway_features_kernel(
         gather_words(0, 1)
         g00 = new_grouped()
         round_w1(g00, raw00, 0, P, "scalar")
-        v_s = [keep.tile([P, S], U8, name="v_s%d" % a, align_bytes=64) for a in range(K_PASSES)]
-        for a in range(K_PASSES):
-            nc.vector.tensor_copy(v_s[a][:], tab_s[:, a, :].indirect(offs_t[:]))
+        v_s = keep.tile([P, S], U8, name="v_s", align_bytes=64)
+        nc.vector.tensor_copy(v_s[:], tab_s[:].indirect(offs_t[:]))
         w2_w = keep.tile([P, R_PASSES, 2 * N], U8, name="w2_w", align_bytes=64)
         nc.vector.tensor_copy(
-            w2_w[:].bitcast(U16).rearrange("p a (t q) -> p a q t", t=PACK),
-            w2_raw[:].bitcast(U16).rearrange("p a (q t) -> p a q t", t=PACK),
+            w2_w[:].bitcast(U16).rearrange("p a (t q) -> p t a q", t=PACK),
+            w2_raw[:].bitcast(U16).rearrange("p a (q t) -> p t a q", t=PACK),
         )
         w2_s = keep.tile([P, R_PASSES, N], U8, name="w2_s", align_bytes=64)
         nc.vector.tensor_copy(
-            w2_s[:].rearrange("p a (t q) -> p a q t", t=PACK),
-            w2_s_raw[:].rearrange("p a (q t) -> p a q t", t=PACK),
+            w2_s[:].rearrange("p a (t q) -> p t a q", t=PACK),
+            w2_s_raw[:].rearrange("p a (q t) -> p t a q", t=PACK),
         )
 
         quantize_w1(0, 0, g00)
@@ -125,7 +128,7 @@ def tile_list_slew_sway_features_kernel(
         round_w1(g01, raw01[0], 0, P // 2, "scalar")
         gather_words(1, 1)
         round_w1(g01, raw01[1], P // 2, P, "vector")
-        quantize_w1(0, 1, g01)
+        quantize_w1(0, 1, g01, 2)
 
         later = [(b, a) for b in range(1, R_PASSES) for a in range(K_PASSES)]
         raws = {ba: load_w1(ba[0], ba[1], 0, PASS, "raw", 3) for ba in later}
@@ -162,23 +165,23 @@ def tile_list_slew_sway_features_kernel(
                 bank = psum.tile([P, PACK, CHUNK], F32, name="sway")
                 cols = slice(c0 + c, c0 + c + CHUNK)
                 scols = slice(h * HALF + c0 + c, h * HALF + c0 + c + CHUNK)
-                for t in range(PACK):
-                    tc_ = slice(t * P, (t + 1) * P)
-                    for a in range(K_PASSES):
+                for a in range(K_PASSES):
+                    for t in range(PACK):
+                        tc_ = slice(t * P, (t + 1) * P)
                         nc.tensor.matmul_mx(
                             bank[:, t, :],
                             lhsT=w1_w[b, a][:, tc_].bitcast(E4M3),
                             lhsT_scale=w1_s[b, a][:, tc_],
                             rhs=v_w[a, h][:, cols].bitcast(E4M3),
-                            rhs_scale=v_s[a][:, scols],
-                            start=(a == 0),
-                            stop=(a == K_PASSES - 1),
+                            rhs_scale=v_s[4 * a : P, scols],
+                            start=(a == 0 and t == 0),
+                            stop=(a == K_PASSES - 1 and t == PACK - 1),
                         )
                 nc.scalar.activation(squares[i][:, c : c + CHUNK, :], bank[:].rearrange("p t n -> p n t"), ACT.Square)
 
         def root(i):
             width = steps[i][3]
-            roots[i] = ring.tile([P, width, PACK], F32, name="root")
+            roots[i] = ring.tile([P, width, PACK], F32, name="root", bufs=5)
             nc.scalar.activation(roots[i][:], squares[i][:], ACT.Sqrt, bias=one[:])
 
         def apply_gain(i):
@@ -222,7 +225,7 @@ def tile_list_slew_sway_features_kernel(
                 second(b, h, 0, HALF, b == R_PASSES - 1)
             if done and (b, h) == (2, 0):
                 for t in range(PACK):
-                    nc.scalar.activation(g2[t][:, 0:HALF], banks[0, t][:], ACT.Identity, bias=neg_rest[:, t : t + 1])
+                    nc.vector.tensor_scalar(g2[t][:, 0:HALF], banks[0, t][:], rest_t[:, t : t + 1], None, ALU.subtract)
                 second(0, 1, 0, HALF, False)
 
         n_steps = len(steps)

@@ -32,113 +32,110 @@ def tile_list_slew_sway_features_kernel(
     with ExitStack() as ctx:
         keep = ctx.enter_context(tc.tile_pool(name="keep", bufs=1))
         ring = ctx.enter_context(tc.tile_pool(name="ring", bufs=3))
-        psum = ctx.enter_context(tc.psum_pool(name="psum", bufs=4))
+        early = ctx.enter_context(tc.tile_pool(name="early", bufs=1))
+        late = ctx.enter_context(tc.tile_pool(name="late", bufs=1))
+        psum = ctx.enter_context(tc.psum_pool(name="psum", bufs=8))
 
         offs_t = keep.tile([P, S // 16], U16, name="offs_t")
         nc.sync.dma_start(offs_t[:], offs)
+        pos1_t = keep.tile([P, PAIRS // 16], U16, name="pos1_t")
+        nc.sync.dma_start(pos1_t[:], pos1)
+        pos2_t = keep.tile([P, PAIRS // 16], U16, name="pos2_t")
+        nc.sync.dma_start(pos2_t[:], pos2)
 
         tab_s = keep.tile([P, T], U8, name="tab_s", align_bytes=64)
-        nc.vector.memset(tab_s[:].bitcast(I32), 0)
-        w2_s_raw = keep.tile([P, R_PASSES, N], U8, name="w2_s_raw", align_bytes=64)
-        nc.gpsimd.memset(w2_s_raw[:].bitcast(I32), 0)
+        nc.sync.dma_start(tab_s[0:32, :].bitcast(I32), tab_scales.rearrange("a q t -> (a q) t").bitcast(I32))
+        nc.vector.memset(tab_s[32:64, :].bitcast(I32), 0)
+        nc.vector.memset(tab_s[64:P, :].bitcast(I32), 0)
+        v_s = keep.tile([P, S], U8, name="v_s", align_bytes=64)
+        nc.vector.memset(v_s[:].bitcast(I32), 0)
         one_in = keep.tile([P, 1], F32, name="one_in")
-        nc.gpsimd.memset(one_in[:], 1.0)
+        nc.vector.memset(one_in[:], 1.0)
         one = keep.tile([P, 1], F32, name="one")
         nc.scalar.activation(one[:], one_in[:], ACT.Sqrt)
 
-        tab_w = [keep.tile([P, T], I32, name="tab_w%d" % a, align_bytes=64) for a in range(K_PASSES)]
+        tab_w = [
+            early.tile([P, T], I32, name="tab_w0", align_bytes=64, offset=0),
+            late.tile([P, T], I32, name="tab_w1", align_bytes=64, offset=0),
+        ]
 
         def load_tab(a):
             nc.sync.dma_start(tab_w[a][:], tab_words[a].rearrange("p t i -> p (t i)").bitcast(I32))
 
-        def load_w1(b, a, c0, width, tag, bufs):
-            raw = ring.tile([P, PACK, width], F32, name=tag, tag=tag, bufs=bufs)
-            rows = w1[a * PASS : (a + 1) * PASS, b * PASS + c0 : b * PASS + c0 + width]
+        def load_w1(b, a):
+            if b == 1:
+                raw = early.tile([P, PACK, PASS], F32, name="raw1%d" % a, align_bytes=64, offset=8192 * a)
+            else:
+                raw = ring.tile([P, PACK, PASS], F32, name="raw", bufs=2)
+            rows = w1[a * PASS : (a + 1) * PASS, b * PASS : (b + 1) * PASS]
             nc.sync.dma_start(raw[:], rows.rearrange("(p j) c -> p j c", j=PACK))
             return raw
 
         load_tab(0)
-        for q in range(4):
-            nc.sync.dma_start(
-                tab_s[32 * q : 32 * q + 8, :].bitcast(I32),
-                tab_scales[:, 4 * q : 4 * q + 4, :].bitcast(I32),
-            )
-        w2_raw = keep.tile([P, R_PASSES, 2 * N], U8, name="w2_raw", align_bytes=64)
-        nc.sync.dma_start(w2_raw[:].bitcast(I32), w2_words.rearrange("a p c -> p a c").bitcast(I32))
-        raw00 = load_w1(0, 0, 0, PASS, "raw", 3)
-        for q in range(4):
-            nc.sync.dma_start(
-                w2_s_raw[32 * q : 32 * q + 4, :, :].bitcast(I32),
-                w2_scales[:, 4 * q : 4 * q + 4, :].rearrange("a r c -> r a c").bitcast(I32),
-            )
+        raw00 = load_w1(0, 0)
+        raw01 = load_w1(0, 1)
         load_tab(1)
-        raw01 = [load_w1(0, 1, i * PASS // 2, PASS // 2, "raw_half%d" % i, 1) for i in range(2)]
         gain_t = keep.tile([P, R_PASSES, PACK], F32, name="gain_t")
-        nc.sync.dma_start(gain_t[:], gain.rearrange("(b p t) -> p b t", p=P, t=PACK))
+        nc.gpsimd.dma_start(gain_t[:], gain.rearrange("(b p t) -> p b t", p=P, t=PACK))
+
+        picked_s = keep.tile([P, S], U8, name="picked_s", align_bytes=64)
+        nc.vector.tensor_copy(picked_s[:], tab_s[:].indirect(offs_t[:]))
+        for a, queue in enumerate((nc.scalar, nc.gpsimd)):
+            for q in range(4):
+                queue.dma_start(
+                    v_s[32 * q + 4 * a : 32 * q + 4 * a + 4, :].bitcast(I32),
+                    picked_s[16 * a + 4 * q : 16 * a + 4 * q + 4, :].bitcast(I32),
+                )
 
         v_w = {}
 
         def gather_words(a, h):
-            v_w[a, h] = keep.tile([P, HALF], U32, name="v_w%d%d" % (a, h), align_bytes=64)
+            if h == 0:
+                v_w[a] = keep.tile([P, S], U32, name="v_w%d" % a, tag="v_w%d" % a, align_bytes=64)
             cols = slice(h * HALF // 16, (h + 1) * HALF // 16)
-            nc.vector.tensor_copy(v_w[a, h][:], tab_w[a][:].bitcast(U32).indirect(offs_t[:, cols]))
+            nc.vector.tensor_copy(v_w[a][:, h * HALF : (h + 1) * HALF], tab_w[a][:].bitcast(U32).indirect(offs_t[:, cols]))
 
         w1_w, w1_s = {}, {}
 
-        def round_w1(grouped, raw, m0, m1, engine):
-            dst = grouped[:].rearrange("p (u v m j) -> p m u j v", u=2, v=2, j=PACK)[:, m0:m1]
+        def round_w1(grouped, raw, engine):
+            dst = grouped[:].rearrange("p (u v m j) -> p m u j v", u=2, v=2, j=PACK)
             src = raw[:].rearrange("p j (m u v) -> p m u j v", u=2, v=2)
             if engine == "scalar":
                 nc.scalar.copy(dst, src)
             else:
                 nc.vector.tensor_copy(dst, src)
 
-        def quantize_w1(b, a, grouped, pieces=1):
+        def quantize_w1(b, a, grouped):
             w1_w[b, a] = keep.tile([P, PASS], U32, name="w1_w%d%d" % (b, a), align_bytes=64)
             w1_s[b, a] = keep.tile([P, PASS], U8, name="w1_s%d%d" % (b, a), align_bytes=64)
-            width = PASS // pieces
-            for c in range(0, PASS, width):
-                nc.vector.quantize_mx(
-                    w1_w[b, a][:, c : c + width].bitcast(E4M3), w1_s[b, a][:, c : c + width], grouped[:, PACK * c : PACK * (c + width)]
-                )
+            nc.vector.quantize_mx(w1_w[b, a][:].bitcast(E4M3), w1_s[b, a][:], grouped[:])
 
-        def new_grouped():
-            return ring.tile([P, PACK * PASS], BF16, name="grouped", align_bytes=64)
 
         gather_words(0, 0)
         gather_words(0, 1)
-        g00 = new_grouped()
-        round_w1(g00, raw00, 0, P, "scalar")
-        v_s = keep.tile([P, S], U8, name="v_s", align_bytes=64)
-        nc.vector.tensor_copy(v_s[:], tab_s[:].indirect(offs_t[:]))
-        w2_w = keep.tile([P, R_PASSES, 2 * N], U8, name="w2_w", align_bytes=64)
-        nc.vector.tensor_copy(
-            w2_w[:].bitcast(U16).rearrange("p a (t q) -> p t a q", t=PACK),
-            w2_raw[:].bitcast(U16).rearrange("p a (q t) -> p t a q", t=PACK),
-        )
-        w2_s = keep.tile([P, R_PASSES, N], U8, name="w2_s", align_bytes=64)
-        nc.vector.tensor_copy(
-            w2_s[:].rearrange("p a (t q) -> p t a q", t=PACK),
-            w2_s_raw[:].rearrange("p a (q t) -> p t a q", t=PACK),
-        )
-
+        g00 = keep.tile([P, PACK * PASS], BF16, name="g00", align_bytes=64)
+        round_w1(g00, raw00, "scalar")
+        g01 = keep.tile([P, PACK * PASS], BF16, name="g01", tag="v_w1", align_bytes=64)
+        round_w1(g01, raw01, "vector")
         quantize_w1(0, 0, g00)
+        quantize_w1(0, 1, g01)
         gather_words(1, 0)
-        g01 = new_grouped()
-        round_w1(g01, raw01[0], 0, P // 2, "scalar")
         gather_words(1, 1)
-        round_w1(g01, raw01[1], P // 2, P, "vector")
-        quantize_w1(0, 1, g01, 2)
 
         later = [(b, a) for b in range(1, R_PASSES) for a in range(K_PASSES)]
-        raws = {ba: load_w1(ba[0], ba[1], 0, PASS, "raw", 3) for ba in later}
-        pos1_t = keep.tile([P, PAIRS // 16], U16, name="pos1_t")
-        nc.sync.dma_start(pos1_t[:], pos1)
-        pos2_t = keep.tile([P, PAIRS // 16], U16, name="pos2_t")
-        nc.sync.dma_start(pos2_t[:], pos2)
-        rest_t = keep.tile([P, PACK], F32, name="rest_t")
+        raws = {ba: load_w1(ba[0], ba[1]) for ba in later}
+        w2_raw = late.tile([P, R_PASSES, 2 * N], U8, name="w2_raw", align_bytes=64, offset=0)
+        nc.sync.dma_start(w2_raw[:].bitcast(I32), w2_words.rearrange("a p c -> p a c").bitcast(I32))
+        w2_s_raw = late.tile([P, R_PASSES, N], U8, name="w2_s_raw", align_bytes=64, offset=4096)
+        nc.vector.memset(w2_s_raw[:].bitcast(I32), 0)
+        for q in range(4):
+            nc.sync.dma_start(
+                w2_s_raw[32 * q : 32 * q + 4, :, :].bitcast(I32),
+                w2_scales[:, 4 * q : 4 * q + 4, :].rearrange("a r c -> r a c").bitcast(I32),
+            )
+        rest_t = late.tile([P, PACK], F32, name="rest_t", align_bytes=64, offset=6144)
         nc.sync.dma_start(rest_t[:], rest.rearrange("(p t) -> p t", t=PACK))
-        ratio_t = keep.tile([P, PACK], F32, name="ratio_t")
+        ratio_t = late.tile([P, PACK], F32, name="ratio_t", align_bytes=64, offset=6144 + 64)
         nc.sync.dma_start(ratio_t[:], ratio.rearrange("(p t) -> p t", t=PACK))
         neg_rest = keep.tile([P, PACK], F32, name="neg_rest")
         nc.gpsimd.tensor_scalar(neg_rest[:], rest_t[:], -1.0, 0.0, ALU.mult, ALU.add)
@@ -148,22 +145,21 @@ def tile_list_slew_sway_features_kernel(
         g2 = [keep.tile([P, S], F32, name="g2_%d" % t) for t in range(PACK)]
 
         steps = []
-        for b, h in ((0, 0), (0, 1), (1, 0), (2, 0), (1, 1), (2, 1)):
-            steps.append((b, h, 0, 2 * CHUNK))
-            if (b, h) == (2, 1):
-                steps.append((b, h, 2 * CHUNK, CHUNK))
-                steps.append((b, h, 3 * CHUNK, CHUNK))
-            else:
-                steps.append((b, h, 2 * CHUNK, 2 * CHUNK))
+        order = ((0, 0), (0, 1), (1, 0), (2, 0), (1, 1), (2, 1))
+        for b, h in order:
+            widths = (256, 128, 128) if (b, h) == order[-1] else (256, 256)
+            c0 = 0
+            for width in widths:
+                steps.append((b, h, c0, width))
+                c0 = c0 + width
 
         squares, roots, rounded = {}, {}, {}
 
         def square(i):
             b, h, c0, width = steps[i]
-            squares[i] = ring.tile([P, width, PACK], F32, name="sq")
+            squares[i] = ring.tile([P, width, PACK], F32, name="sq", bufs=3)
             for c in range(0, width, CHUNK):
-                bank = psum.tile([P, PACK, CHUNK], F32, name="sway")
-                cols = slice(c0 + c, c0 + c + CHUNK)
+                bank = psum.tile([P, PACK, CHUNK], F32, name="sway", tag="bank")
                 scols = slice(h * HALF + c0 + c, h * HALF + c0 + c + CHUNK)
                 for a in range(K_PASSES):
                     for t in range(PACK):
@@ -172,7 +168,7 @@ def tile_list_slew_sway_features_kernel(
                             bank[:, t, :],
                             lhsT=w1_w[b, a][:, tc_].bitcast(E4M3),
                             lhsT_scale=w1_s[b, a][:, tc_],
-                            rhs=v_w[a, h][:, cols].bitcast(E4M3),
+                            rhs=v_w[a][:, scols].bitcast(E4M3),
                             rhs_scale=v_s[4 * a : P, scols],
                             start=(a == 0 and t == 0),
                             stop=(a == K_PASSES - 1 and t == PACK - 1),
@@ -180,71 +176,103 @@ def tile_list_slew_sway_features_kernel(
                 nc.scalar.activation(squares[i][:, c : c + CHUNK, :], bank[:].rearrange("p t n -> p n t"), ACT.Square)
 
         def root(i):
-            width = steps[i][3]
-            roots[i] = ring.tile([P, width, PACK], F32, name="root", bufs=5)
-            nc.scalar.activation(roots[i][:], squares[i][:], ACT.Sqrt, bias=one[:])
+            b, h, c0, width = steps[i]
+            if c0 == 0:
+                roots[b, h] = ring.tile([P, HALF, PACK], F32, name="root", bufs=5)
+            nc.scalar.activation(roots[b, h][:, c0 : c0 + width, :], squares[i][:], ACT.Sqrt, bias=one[:])
+
+        def piece(i):
+            b, h, c0, width = steps[i]
+            if (b, h) in order[-2:]:
+                return slice(c0, c0 + width)
+            return slice(0, HALF) if c0 + width == HALF else None
 
         def apply_gain(i):
-            b, h, c0, width = steps[i]
-            rounded[i] = ring.tile([P, width, PACK], BF16, name="h_bf", align_bytes=64)
-            nc.vector.tensor_tensor(
-                rounded[i][:], roots[i][:], gain_t[:, b : b + 1, :].broadcast_to([P, width, PACK]), ALU.mult
-            )
-
-        def quantize_h(i):
-            b, h, c0, width = steps[i]
-            cols = slice(c0, c0 + width)
-            nc.vector.quantize_mx(
-                h_w[b, h][:, cols].bitcast(E4M3), h_s[b, h][:, cols], rounded[i][:].rearrange("p n t -> p (n t)")
-            )
-
-        banks = {}
-
-        def second(b, h, c0, width, last):
-            cols = slice(c0, c0 + width)
-            for t in range(PACK):
-                if b == 0:
-                    banks[h, t] = psum.tile([P, HALF], F32, name="feat")
-                nc.tensor.matmul_mx(
-                    banks[h, t][:, cols],
-                    lhsT=w2_w[:, b, 2 * t * P : 2 * (t + 1) * P].bitcast(E2M1),
-                    lhsT_scale=w2_s[:, b, t * P : (t + 1) * P],
-                    rhs=h_w[b, h][:, cols].bitcast(E4M3),
-                    rhs_scale=h_s[b, h][:, cols],
-                    start=(b == 0),
-                    stop=last,
+            b, h = steps[i][:2]
+            cols = piece(i)
+            if cols is not None:
+                width = cols.stop - cols.start
+                rounded[i] = ring.tile([P, width, PACK], BF16, name="h_bf", align_bytes=64)
+                nc.vector.tensor_tensor(
+                    rounded[i][:], roots[b, h][:, cols, :], gain_t[:, b : b + 1, :].broadcast_to([P, width, PACK]), ALU.mult
                 )
 
-        def after_quantize(i):
-            b, h, c0, width = steps[i]
-            done = c0 + width == HALF
-            if (b, h) == (2, 1):
-                for c in range(c0, c0 + width, CHUNK):
-                    second(b, h, c, CHUNK, c + CHUNK == HALF)
-            elif done and (b, h) != (0, 1):
-                second(b, h, 0, HALF, b == R_PASSES - 1)
-            if done and (b, h) == (2, 0):
-                for t in range(PACK):
-                    nc.vector.tensor_scalar(g2[t][:, 0:HALF], banks[0, t][:], rest_t[:, t : t + 1], None, ALU.subtract)
-                second(0, 1, 0, HALF, False)
+        def quantize_h(i):
+            b, h = steps[i][:2]
+            cols = piece(i)
+            if cols is not None:
+                nc.vector.quantize_mx(
+                    h_w[b, h][:, cols].bitcast(E4M3), h_s[b, h][:, cols], rounded[i][:].rearrange("p n t -> p (n t)")
+                )
+
+        def deal_w2():
+            w2_w = late.tile([P, R_PASSES, 2 * N], U8, name="w2_w", align_bytes=64, offset=8192)
+            nc.vector.tensor_copy(
+                w2_w[:].bitcast(U16).rearrange("p a (t q) -> p t a q", t=PACK),
+                w2_raw[:].bitcast(U16).rearrange("p a (q t) -> p t a q", t=PACK),
+            )
+            w2_s = late.tile([P, R_PASSES, N], U8, name="w2_s", align_bytes=64, offset=12288)
+            nc.vector.tensor_copy(
+                w2_s[:].rearrange("p a (t q) -> p t a q", t=PACK),
+                w2_s_raw[:].rearrange("p a (q t) -> p t a q", t=PACK),
+            )
+            return w2_w, w2_s
+
+        banks = {}
+        w2 = []
+
+        def second(t, b, h, c0, width):
+            cols = slice(c0, c0 + width)
+            if b == 0:
+                banks[h, t] = psum.tile([P, HALF], F32, name="feat", tag="bank")
+            nc.tensor.matmul_mx(
+                banks[h, t][:, cols],
+                lhsT=w2[0][:, b, 2 * t * P : 2 * (t + 1) * P].bitcast(E2M1),
+                lhsT_scale=w2[1][:, b, t * P : (t + 1) * P],
+                rhs=h_w[b, h][:, cols].bitcast(E4M3),
+                rhs_scale=h_s[b, h][:, cols],
+                start=(b == 0),
+                stop=(b == R_PASSES - 1 and c0 + width == HALF),
+            )
+
+        def first_half_features(t):
+            for b in range(R_PASSES):
+                second(t, b, 0, 0, HALF)
+            if t % 2 == 0:
+                nc.vector.tensor_scalar(g2[t][:, 0:HALF], banks[0, t][:], rest_t[:, t : t + 1], None, ALU.subtract)
+            else:
+                nc.scalar.activation(g2[t][:, 0:HALF], banks[0, t][:], ACT.Identity, bias=neg_rest[:, t : t + 1])
 
         n_steps = len(steps)
-        for i in range(n_steps + 3):
+        for i in range(n_steps + 2):
             if i < n_steps:
                 square(i)
             if 1 <= i <= n_steps:
                 root(i - 1)
-            if 2 <= i <= n_steps + 1:
-                apply_gain(i - 2)
-            if 1 <= i <= len(later):
-                b, a = later[i - 1]
-                grouped = new_grouped()
-                round_w1(grouped, raws[b, a], 0, P, "vector")
-            if i >= 3:
-                quantize_h(i - 3)
-                after_quantize(i - 3)
-            if 1 <= i <= len(later):
+            if i < len(later):
+                b, a = later[i]
+                grouped = late.tile([P, PACK * PASS], BF16, name="grouped%d" % i, align_bytes=64, offset=8192 + 4096 * a)
+                round_w1(grouped, raws[b, a], "vector")
+            if 1 <= i <= n_steps:
+                apply_gain(i - 1)
+            if i < len(later):
                 quantize_w1(b, a, grouped)
+            if i == len(later):
+                w2.extend(deal_w2())
+            if i >= 2:
+                quantize_h(i - 2)
+            if i in (10, 11):
+                first_half_features(2 * (i - 10))
+                first_half_features(2 * (i - 10) + 1)
+            if i == 12:
+                for b in range(R_PASSES - 1):
+                    for t in range(PACK):
+                        second(t, b, 1, 0, HALF)
+            if i >= 12:
+                b, h, c0, width = steps[i - 2]
+                for c in range(c0, c0 + width, CHUNK):
+                    for t in range(PACK):
+                        second(t, b, h, c, CHUNK)
 
         for t in range(PACK):
             nc.scalar.activation(g2[t][:, HALF:S], banks[1, t][:], ACT.Identity, bias=neg_rest[:, t : t + 1])
@@ -254,30 +282,52 @@ def tile_list_slew_sway_features_kernel(
         part = PAIRS // 2
         y_rows = out_0.rearrange("(p t) m -> p t m", t=PACK)
         words_out = out_1[0].rearrange("p m i -> p (m i)").bitcast(I32)
-        y_bf = []
-        for k in range(2):
-            cols = slice(k * part, (k + 1) * part)
+        y = [keep.tile([P, PACK, part], F32, name="y%d" % k) for k in range(2)]
+        y_bf = [keep.tile([P, PACK * part], BF16, name="y_bf%d" % k, align_bytes=64) for k in range(2)]
+        jibs, hooks = {}, {}
+
+        def pick(k, t):
             lcols = slice(k * part // 16, (k + 1) * part // 16)
-            y = keep.tile([P, PACK, part], F32, name="y%d" % k)
-            for t in range(PACK):
-                jib = ring.tile([P, part], F32, name="jib")
-                nc.vector.tensor_copy(jib[:], g2[t][:].indirect(pos1_t[:, lcols]))
-                hook = ring.tile([P, part], F32, name="hook")
-                nc.vector.tensor_copy(hook[:], g2[t][:].indirect(pos2_t[:, lcols]))
-                if k == 1 and t == 2:
-                    nc.vector.quantize_mx(y_w[:, 0:part].bitcast(E4M3), y_s[:, 0:part], y_bf[0][:])
-                    nc.sync.dma_start(words_out[:, 0:part], y_w[:, 0:part].bitcast(I32))
-                nc.vector.scalar_tensor_tensor(y[:, t, :], hook[:], ratio_t[:, t : t + 1], jib[:], ALU.mult, ALU.max)
-            nc.scalar.dma_start(y_rows[:, :, cols], y[:])
-            y_bf.append(keep.tile([P, PACK * part], BF16, name="y_bf%d" % k, align_bytes=64))
-            dst = y_bf[k][:].rearrange("p (c i t) -> p c t i", i=4, t=PACK)
-            src = y[:].rearrange("p t (c i) -> p c t i", i=4)
-            if k == 0:
+            jibs[k, t] = ring.tile([P, part], F32, name="jib")
+            nc.vector.tensor_copy(jibs[k, t][:], g2[t][:].indirect(pos1_t[:, lcols]))
+            hooks[k, t] = ring.tile([P, part], F32, name="hook")
+            nc.vector.tensor_copy(hooks[k, t][:], g2[t][:].indirect(pos2_t[:, lcols]))
+
+        def round_y(k, t0, t1, engine):
+            dst = y_bf[k][:].rearrange("p (c i t) -> p c t i", i=4, t=PACK)[:, :, t0:t1, :]
+            src = y[k][:].rearrange("p t (c i) -> p c t i", i=4)[:, :, t0:t1, :]
+            if engine == "scalar":
                 nc.scalar.copy(dst, src)
             else:
                 nc.vector.tensor_copy(dst, src)
-        nc.vector.quantize_mx(y_w[:, part:PAIRS].bitcast(E4M3), y_s[:, part:PAIRS], y_bf[1][:])
-        nc.sync.dma_start(words_out[:, part:PAIRS], y_w[:, part:PAIRS].bitcast(I32))
+
+        def quantize_y(k):
+            cols = slice(k * part, (k + 1) * part)
+            nc.vector.quantize_mx(y_w[:, cols].bitcast(E4M3), y_s[:, cols], y_bf[k][:])
+            nc.sync.dma_start(words_out[:, cols], y_w[:, cols].bitcast(I32))
+
+        def larger(k, t):
+            cols = slice(k * part, (k + 1) * part)
+            nc.vector.scalar_tensor_tensor(y[k][:, t, :], hooks[k, t][:], ratio_t[:, t : t + 1], jibs[k, t][:], ALU.mult, ALU.max)
+            if (k, t) == (0, 3):
+                nc.sync.dma_start(y_rows[:, :, cols], y[k][:])
+                round_y(0, 0, 4, "scalar")
+            if (k, t) == (1, 1):
+                round_y(1, 0, 2, "scalar")
+                quantize_y(0)
+            if (k, t) == (1, 2):
+                nc.sync.dma_start(y_rows[:, 0:3, cols], y[k][:, 0:3, :])
+            if (k, t) == (1, 3):
+                nc.scalar.dma_start(y_rows[:, 3, cols], y[k][:, 3, :])
+                round_y(1, 2, 4, "vector")
+                quantize_y(1)
+
+        picks = [(k, t) for k in range(2) for t in range(PACK)]
+        for i in range(len(picks) + 1):
+            if i < len(picks):
+                pick(*picks[i])
+            if i >= 1:
+                larger(*picks[i - 1])
         for q in range(4):
             queue = nc.scalar if q % 2 == 0 else nc.sync
             queue.dma_start(out_2[0, 4 * q : 4 * q + 4, :].bitcast(I32), y_s[32 * q : 32 * q + 4, :].bitcast(I32))

@@ -34,6 +34,7 @@ def tile_list_slew_sway_features_kernel(
         ring = ctx.enter_context(tc.tile_pool(name="ring", bufs=3))
         early = ctx.enter_context(tc.tile_pool(name="early", bufs=1))
         late = ctx.enter_context(tc.tile_pool(name="late", bufs=1))
+        first = ctx.enter_context(tc.tile_pool(name="first", bufs=1))
         psum = ctx.enter_context(tc.psum_pool(name="psum", bufs=8))
 
         offs_t = keep.tile([P, S // 16], U16, name="offs_t")
@@ -62,19 +63,16 @@ def tile_list_slew_sway_features_kernel(
         def load_tab(a):
             nc.sync.dma_start(tab_w[a][:], tab_words[a].rearrange("p t i -> p (t i)").bitcast(I32))
 
-        def load_w1(b, a):
-            if b == 1:
-                raw = early.tile([P, PACK, PASS], F32, name="raw1%d" % a, align_bytes=64, offset=8192 * a)
-            else:
-                raw = ring.tile([P, PACK, PASS], F32, name="raw", bufs=2)
-            rows = w1[a * PASS : (a + 1) * PASS, b * PASS : (b + 1) * PASS]
+        def load_w1(pool, b, a, c0, width, offset):
+            raw = pool.tile([P, PACK, width], F32, name="raw%d%d_%d" % (b, a, c0), align_bytes=64, offset=offset)
+            rows = w1[a * PASS : (a + 1) * PASS, b * PASS + c0 : b * PASS + c0 + width]
             nc.sync.dma_start(raw[:], rows.rearrange("(p j) c -> p j c", j=PACK))
             return raw
 
         load_tab(0)
-        raw00 = load_w1(0, 0)
-        raw01 = load_w1(0, 1)
         load_tab(1)
+        raw00 = load_w1(first, 0, 0, 0, PASS, 0)
+        raw01 = [load_w1(first, 0, 1, i * PASS // 2, PASS // 2, 8192 + 4096 * i) for i in range(2)]
         gain_t = keep.tile([P, R_PASSES, PACK], F32, name="gain_t")
         nc.gpsimd.dma_start(gain_t[:], gain.rearrange("(b p t) -> p b t", p=P, t=PACK))
 
@@ -97,45 +95,53 @@ def tile_list_slew_sway_features_kernel(
 
         w1_w, w1_s = {}, {}
 
-        def round_w1(grouped, raw, engine):
-            dst = grouped[:].rearrange("p (u v m j) -> p m u j v", u=2, v=2, j=PACK)
+        def round_w1(grouped, raw, engine, m0=0, m1=P):
+            dst = grouped[:].rearrange("p (u v m j) -> p m u j v", u=2, v=2, j=PACK)[:, m0:m1]
             src = raw[:].rearrange("p j (m u v) -> p m u j v", u=2, v=2)
             if engine == "scalar":
                 nc.scalar.copy(dst, src)
             else:
                 nc.vector.tensor_copy(dst, src)
 
-        def quantize_w1(b, a, grouped):
+        def quantize_w1(b, a, grouped, pieces=1):
             w1_w[b, a] = keep.tile([P, PASS], U32, name="w1_w%d%d" % (b, a), align_bytes=64)
             w1_s[b, a] = keep.tile([P, PASS], U8, name="w1_s%d%d" % (b, a), align_bytes=64)
-            nc.vector.quantize_mx(w1_w[b, a][:].bitcast(E4M3), w1_s[b, a][:], grouped[:])
+            width = PASS // pieces
+            for c in range(0, PASS, width):
+                nc.vector.quantize_mx(
+                    w1_w[b, a][:, c : c + width].bitcast(E4M3), w1_s[b, a][:, c : c + width], grouped[:, PACK * c : PACK * (c + width)]
+                )
+
+        def new_grouped():
+            return ring.tile([P, PACK * PASS], BF16, name="grouped", tag="grouped", bufs=2, align_bytes=64)
 
 
         gather_words(0, 0)
         gather_words(0, 1)
-        g00 = keep.tile([P, PACK * PASS], BF16, name="g00", align_bytes=64)
-        round_w1(g00, raw00, "scalar")
-        g01 = keep.tile([P, PACK * PASS], BF16, name="g01", tag="v_w1", align_bytes=64)
-        round_w1(g01, raw01, "vector")
-        quantize_w1(0, 0, g00)
-        quantize_w1(0, 1, g01)
         gather_words(1, 0)
         gather_words(1, 1)
+        g00 = new_grouped()
+        round_w1(g00, raw00, "vector")
+        g01 = new_grouped()
+        round_w1(g01, raw01[0], "scalar", 0, P // 2)
+        quantize_w1(0, 0, g00)
+        round_w1(g01, raw01[1], "vector", P // 2, P)
+        quantize_w1(0, 1, g01, 2)
 
         later = [(b, a) for b in range(1, R_PASSES) for a in range(K_PASSES)]
-        raws = {ba: load_w1(ba[0], ba[1]) for ba in later}
-        w2_raw = late.tile([P, R_PASSES, 2 * N], U8, name="w2_raw", align_bytes=64, offset=0)
+        raws = {(b, a): load_w1(early if b == 1 else late, b, a, 0, PASS, 8192 * a) for b, a in later}
+        w2_raw = first.tile([P, R_PASSES, 2 * N], U8, name="w2_raw", align_bytes=64, offset=0)
         nc.sync.dma_start(w2_raw[:].bitcast(I32), w2_words.rearrange("a p c -> p a c").bitcast(I32))
-        w2_s_raw = late.tile([P, R_PASSES, N], U8, name="w2_s_raw", align_bytes=64, offset=4096)
+        w2_s_raw = first.tile([P, R_PASSES, N], U8, name="w2_s_raw", align_bytes=64, offset=4096)
         nc.vector.memset(w2_s_raw[:].bitcast(I32), 0)
         for q in range(4):
             nc.sync.dma_start(
                 w2_s_raw[32 * q : 32 * q + 4, :, :].bitcast(I32),
                 w2_scales[:, 4 * q : 4 * q + 4, :].rearrange("a r c -> r a c").bitcast(I32),
             )
-        rest_t = late.tile([P, PACK], F32, name="rest_t", align_bytes=64, offset=6144)
+        rest_t = first.tile([P, PACK], F32, name="rest_t", align_bytes=64, offset=6144)
         nc.sync.dma_start(rest_t[:], rest.rearrange("(p t) -> p t", t=PACK))
-        ratio_t = late.tile([P, PACK], F32, name="ratio_t", align_bytes=64, offset=6144 + 64)
+        ratio_t = first.tile([P, PACK], F32, name="ratio_t", align_bytes=64, offset=6144 + 64)
         nc.sync.dma_start(ratio_t[:], ratio.rearrange("(p t) -> p t", t=PACK))
         neg_rest = keep.tile([P, PACK], F32, name="neg_rest")
         nc.gpsimd.tensor_scalar(neg_rest[:], rest_t[:], -1.0, 0.0, ALU.mult, ALU.add)
@@ -147,7 +153,7 @@ def tile_list_slew_sway_features_kernel(
         steps = []
         order = ((0, 0), (0, 1), (1, 0), (2, 0), (1, 1), (2, 1))
         for b, h in order:
-            widths = (256, 128, 128) if (b, h) == order[-1] else (256, 256)
+            widths = (128, 128, 128, 128) if (b, h) == order[-1] else (256, 256)
             c0 = 0
             for width in widths:
                 steps.append((b, h, c0, width))
@@ -206,12 +212,12 @@ def tile_list_slew_sway_features_kernel(
                 )
 
         def deal_w2():
-            w2_w = late.tile([P, R_PASSES, 2 * N], U8, name="w2_w", align_bytes=64, offset=8192)
+            w2_w = ring.tile([P, R_PASSES, 2 * N], U8, name="w2_w", tag="grouped", bufs=2, align_bytes=64)
             nc.vector.tensor_copy(
                 w2_w[:].bitcast(U16).rearrange("p a (t q) -> p t a q", t=PACK),
                 w2_raw[:].bitcast(U16).rearrange("p a (q t) -> p t a q", t=PACK),
             )
-            w2_s = late.tile([P, R_PASSES, N], U8, name="w2_s", align_bytes=64, offset=12288)
+            w2_s = ring.tile([P, R_PASSES, N], U8, name="w2_s", tag="grouped", bufs=2, align_bytes=64)
             nc.vector.tensor_copy(
                 w2_s[:].rearrange("p a (t q) -> p t a q", t=PACK),
                 w2_s_raw[:].rearrange("p a (q t) -> p t a q", t=PACK),
@@ -238,7 +244,7 @@ def tile_list_slew_sway_features_kernel(
         def first_half_features(t):
             for b in range(R_PASSES):
                 second(t, b, 0, 0, HALF)
-            if t % 2 == 0:
+            if t != 1:
                 nc.vector.tensor_scalar(g2[t][:, 0:HALF], banks[0, t][:], rest_t[:, t : t + 1], None, ALU.subtract)
             else:
                 nc.scalar.activation(g2[t][:, 0:HALF], banks[0, t][:], ACT.Identity, bias=neg_rest[:, t : t + 1])
@@ -251,7 +257,7 @@ def tile_list_slew_sway_features_kernel(
                 root(i - 1)
             if i < len(later):
                 b, a = later[i]
-                grouped = late.tile([P, PACK * PASS], BF16, name="grouped%d" % i, align_bytes=64, offset=8192 + 4096 * a)
+                grouped = new_grouped()
                 round_w1(grouped, raws[b, a], "vector")
             if 1 <= i <= n_steps:
                 apply_gain(i - 1)
@@ -264,15 +270,13 @@ def tile_list_slew_sway_features_kernel(
             if i in (10, 11):
                 first_half_features(2 * (i - 10))
                 first_half_features(2 * (i - 10) + 1)
-            if i == 12:
-                for b in range(R_PASSES - 1):
-                    for t in range(PACK):
-                        second(t, b, 1, 0, HALF)
-            if i >= 12:
-                b, h, c0, width = steps[i - 2]
-                for c in range(c0, c0 + width, CHUNK):
-                    for t in range(PACK):
-                        second(t, b, h, c, CHUNK)
+            if i in (12, 13):
+                for t in range(PACK):
+                    second(t, i - 12, 1, 0, HALF)
+            for j in {13: (10, 11), 14: (12,), 15: (13,)}.get(i, ()):
+                b, h, c0, width = steps[j]
+                for t in range(PACK):
+                    second(t, b, h, c0, width)
 
         for t in range(PACK):
             nc.scalar.activation(g2[t][:, HALF:S], banks[1, t][:], ACT.Identity, bias=neg_rest[:, t : t + 1])
@@ -282,52 +286,46 @@ def tile_list_slew_sway_features_kernel(
         part = PAIRS // 2
         y_rows = out_0.rearrange("(p t) m -> p t m", t=PACK)
         words_out = out_1[0].rearrange("p m i -> p (m i)").bitcast(I32)
-        y = [keep.tile([P, PACK, part], F32, name="y%d" % k) for k in range(2)]
-        y_bf = [keep.tile([P, PACK * part], BF16, name="y_bf%d" % k, align_bytes=64) for k in range(2)]
+        y = keep.tile([P, PACK, PAIRS], F32, name="y")
+        y_bf = keep.tile([P, PAIRS * PACK], BF16, name="y_bf", align_bytes=64)
+        halves = (slice(0, part), slice(part, PAIRS))
+        picks = [(t, slice(0, PAIRS)) for t in range(PACK - 1)] + [(PACK - 1, cols) for cols in halves]
         jibs, hooks = {}, {}
 
-        def pick(k, t):
-            lcols = slice(k * part // 16, (k + 1) * part // 16)
-            jibs[k, t] = ring.tile([P, part], F32, name="jib")
-            nc.vector.tensor_copy(jibs[k, t][:], g2[t][:].indirect(pos1_t[:, lcols]))
-            hooks[k, t] = ring.tile([P, part], F32, name="hook")
-            nc.vector.tensor_copy(hooks[k, t][:], g2[t][:].indirect(pos2_t[:, lcols]))
+        def pick(i):
+            t, cols = picks[i]
+            lcols = slice(cols.start // 16, cols.stop // 16)
+            jibs[i] = ring.tile([P, cols.stop - cols.start], F32, name="jib")
+            nc.vector.tensor_copy(jibs[i][:], g2[t][:].indirect(pos1_t[:, lcols]))
+            hooks[i] = ring.tile([P, cols.stop - cols.start], F32, name="hook")
+            nc.vector.tensor_copy(hooks[i][:], g2[t][:].indirect(pos2_t[:, lcols]))
 
-        def round_y(k, t0, t1, engine):
-            dst = y_bf[k][:].rearrange("p (c i t) -> p c t i", i=4, t=PACK)[:, :, t0:t1, :]
-            src = y[k][:].rearrange("p t (c i) -> p c t i", i=4)[:, :, t0:t1, :]
-            if engine == "scalar":
-                nc.scalar.copy(dst, src)
-            else:
-                nc.vector.tensor_copy(dst, src)
+        def larger(i):
+            t, cols = picks[i]
+            nc.vector.scalar_tensor_tensor(y[:, t, cols], hooks[i][:], ratio_t[:, t : t + 1], jibs[i][:], ALU.mult, ALU.max)
+            nc.sync.dma_start(y_rows[:, t, cols], y[:, t, cols])
 
-        def quantize_y(k):
-            cols = slice(k * part, (k + 1) * part)
-            nc.vector.quantize_mx(y_w[:, cols].bitcast(E4M3), y_s[:, cols], y_bf[k][:])
-            nc.sync.dma_start(words_out[:, cols], y_w[:, cols].bitcast(I32))
+        def round_y(copy, t0, cols):
+            groups = slice(cols.start // 4, cols.stop // 4)
+            dst = y_bf[:].rearrange("p (c i t) -> p c t i", i=4, t=PACK)[:, groups, t0 : t0 + 2, :]
+            src = y[:].rearrange("p t (c i) -> p c t i", i=4)[:, groups, t0 : t0 + 2, :]
+            copy(dst, src)
 
-        def larger(k, t):
-            cols = slice(k * part, (k + 1) * part)
-            nc.vector.scalar_tensor_tensor(y[k][:, t, :], hooks[k, t][:], ratio_t[:, t : t + 1], jibs[k, t][:], ALU.mult, ALU.max)
-            if (k, t) == (0, 3):
-                nc.sync.dma_start(y_rows[:, :, cols], y[k][:])
-                round_y(0, 0, 4, "scalar")
-            if (k, t) == (1, 1):
-                round_y(1, 0, 2, "scalar")
-                quantize_y(0)
-            if (k, t) == (1, 2):
-                nc.sync.dma_start(y_rows[:, 0:3, cols], y[k][:, 0:3, :])
-            if (k, t) == (1, 3):
-                nc.scalar.dma_start(y_rows[:, 3, cols], y[k][:, 3, :])
-                round_y(1, 2, 4, "vector")
-                quantize_y(1)
+        def quantize_y(cols):
+            nc.vector.quantize_mx(y_w[:, cols].bitcast(E4M3), y_s[:, cols], y_bf[:, PACK * cols.start : PACK * cols.stop])
+            nc.scalar.dma_start(words_out[:, cols], y_w[:, cols].bitcast(I32))
 
-        picks = [(k, t) for k in range(2) for t in range(PACK)]
-        for i in range(len(picks) + 1):
-            if i < len(picks):
-                pick(*picks[i])
-            if i >= 1:
-                larger(*picks[i - 1])
+        pick(0)
+        for i in range(1, len(picks)):
+            pick(i)
+            larger(i - 1)
+            if i == 2:
+                round_y(nc.scalar.copy, 0, slice(0, PAIRS))
+        round_y(nc.scalar.copy, 2, halves[0])
+        larger(len(picks) - 1)
+        quantize_y(halves[0])
+        round_y(nc.vector.tensor_copy, 2, halves[1])
+        quantize_y(halves[1])
         for q in range(4):
-            queue = nc.scalar if q % 2 == 0 else nc.sync
+            queue = nc.sync if q < 3 else nc.scalar
             queue.dma_start(out_2[0, 4 * q : 4 * q + 4, :].bitcast(I32), y_s[32 * q : 32 * q + 4, :].bitcast(I32))

from contextlib import ExitStack

import concourse.mybir as mybir

T, S, PAIRS, K, H, N = 4096, 1024, 512, 1024, 1536, 512
FLOPS = 2 * K * H * S + 2 * H * N * S

F32 = mybir.dt.float32
BF16 = mybir.dt.bfloat16
I32 = mybir.dt.int32
U32 = mybir.dt.uint32
U16 = mybir.dt.uint16
U8 = mybir.dt.uint8
E4M3 = mybir.dt.float8_e4m3fn_x4
E2M1 = mybir.dt.float4_e2m1fn_x4
ACT = mybir.ActivationFunctionType
ALU = mybir.AluOpType

P = 128
PACK = 4
PASS = P * PACK
K_PASSES = K // PASS
R_PASSES = H // PASS
HALF = S // 2
CHUNK = 128


def tile_list_slew_sway_features_kernel(
    tc, tab_words, tab_scales, offs, w1, gain, w2_words, w2_scales, rest, ratio, pos1, pos2, out_0, out_1, out_2
):
    nc = tc.nc
    with ExitStack() as ctx:
        keep = ctx.enter_context(tc.tile_pool(name="keep", bufs=1))
        ring = ctx.enter_context(tc.tile_pool(name="ring", bufs=3))
        early = ctx.enter_context(tc.tile_pool(name="early", bufs=1))
        late = ctx.enter_context(tc.tile_pool(name="late", bufs=1))
        first = ctx.enter_context(tc.tile_pool(name="first", bufs=1))
        psum = ctx.enter_context(tc.psum_pool(name="psum", bufs=8))

        offs_t = keep.tile([P, S // 16], U16, name="offs_t")
        nc.sync.dma_start(offs_t[:], offs)
        pos1_t = keep.tile([P, PAIRS // 16], U16, name="pos1_t")
        nc.sync.dma_start(pos1_t[:], pos1)
        pos2_t = keep.tile([P, PAIRS // 16], U16, name="pos2_t")
        nc.sync.dma_start(pos2_t[:], pos2)

        tab_s = keep.tile([P, T], U8, name="tab_s", align_bytes=64)
        nc.sync.dma_start(tab_s[0:32, :].bitcast(I32), tab_scales.rearrange("a q t -> (a q) t").bitcast(I32))
        nc.vector.memset(tab_s[32:64, :].bitcast(I32), 0)
        nc.vector.memset(tab_s[64:P, :].bitcast(I32), 0)
        v_s = keep.tile([P, S], U8, name="v_s", align_bytes=64)
        nc.vector.memset(v_s[:].bitcast(I32), 0)
        one_in = keep.tile([P, 1], F32, name="one_in")
        nc.vector.memset(one_in[:], 1.0)
        one = keep.tile([P, 1], F32, name="one")
        nc.scalar.activation(one[:], one_in[:], ACT.Sqrt)

        tab_w = [
            early.tile([P, T], I32, name="tab_w0", align_bytes=64, offset=0),
            late.tile([P, T], I32, name="tab_w1", align_bytes=64, offset=0),
        ]

        def load_tab(a):
            nc.sync.dma_start(tab_w[a][:], tab_words[a].rearrange("p t i -> p (t i)").bitcast(I32))

        def load_w1(pool, b, a, c0, width, offset):
            raw = pool.tile([P, PACK, width], F32, name="raw%d%d_%d" % (b, a, c0), align_bytes=64, offset=offset)
            rows = w1[a * PASS : (a + 1) * PASS, b * PASS + c0 : b * PASS + c0 + width]
            nc.sync.dma_start(raw[:], rows.rearrange("(p j) c -> p j c", j=PACK))
            return raw

        load_tab(0)
        load_tab(1)
        raw00 = load_w1(first, 0, 0, 0, PASS, 0)
        raw01 = [load_w1(first, 0, 1, i * PASS // 2, PASS // 2, 8192 + 4096 * i) for i in range(2)]
        gain_t = keep.tile([P, R_PASSES, PACK], F32, name="gain_t")
        nc.gpsimd.dma_start(gain_t[:], gain.rearrange("(b p t) -> p b t", p=P, t=PACK))

        picked_s = keep.tile([P, S], U8, name="picked_s", align_bytes=64)
        nc.vector.tensor_copy(picked_s[:], tab_s[:].indirect(offs_t[:]))
        for a, queue in enumerate((nc.scalar, nc.gpsimd)):
            for q in range(4):
                queue.dma_start(
                    v_s[32 * q + 4 * a : 32 * q + 4 * a + 4, :].bitcast(I32),
                    picked_s[16 * a + 4 * q : 16 * a + 4 * q + 4, :].bitcast(I32),
                )

        v_w = {}

        def gather_words(a, h):
            if h == 0:
                v_w[a] = keep.tile([P, S], U32, name="v_w%d" % a, tag="v_w%d" % a, align_bytes=64)
            cols = slice(h * HALF // 16, (h + 1) * HALF // 16)
            nc.vector.tensor_copy(v_w[a][:, h * HALF : (h + 1) * HALF], tab_w[a][:].bitcast(U32).indirect(offs_t[:, cols]))

        w1_w, w1_s = {}, {}

        def round_w1(grouped, raw, engine, m0=0, m1=P):
            dst = grouped[:].rearrange("p (u v m j) -> p m u j v", u=2, v=2, j=PACK)[:, m0:m1]
            src = raw[:].rearrange("p j (m u v) -> p m u j v", u=2, v=2)
            if engine == "scalar":
                nc.scalar.copy(dst, src)
            else:
                nc.vector.tensor_copy(dst, src)

        def quantize_w1(b, a, grouped, pieces=1):
            w1_w[b, a] = keep.tile([P, PASS], U32, name="w1_w%d%d" % (b, a), align_bytes=64)
            w1_s[b, a] = keep.tile([P, PASS], U8, name="w1_s%d%d" % (b, a), align_bytes=64)
            width = PASS // pieces
            for c in range(0, PASS, width):
                nc.vector.quantize_mx(
                    w1_w[b, a][:, c : c + width].bitcast(E4M3), w1_s[b, a][:, c : c + width], grouped[:, PACK * c : PACK * (c + width)]
                )

        def new_grouped():
            return ring.tile([P, PACK * PASS], BF16, name="grouped", tag="grouped", bufs=2, align_bytes=64)


        gather_words(0, 0)
        gather_words(0, 1)
        gather_words(1, 0)
        gather_words(1, 1)
        g00 = new_grouped()
        round_w1(g00, raw00, "vector")
        g01 = new_grouped()
        round_w1(g01, raw01[0], "scalar", 0, P // 2)
        quantize_w1(0, 0, g00)
        round_w1(g01, raw01[1], "vector", P // 2, P)
        quantize_w1(0, 1, g01, 2)

        later = [(b, a) for b in range(1, R_PASSES) for a in range(K_PASSES)]
        raws = {(b, a): load_w1(early if b == 1 else late, b, a, 0, PASS, 8192 * a) for b, a in later}
        w2_raw = first.tile([P, R_PASSES, 2 * N], U8, name="w2_raw", align_bytes=64, offset=0)
        nc.sync.dma_start(w2_raw[:].bitcast(I32), w2_words.rearrange("a p c -> p a c").bitcast(I32))
        w2_s_raw = first.tile([P, R_PASSES, N], U8, name="w2_s_raw", align_bytes=64, offset=4096)
        nc.vector.memset(w2_s_raw[:].bitcast(I32), 0)
        for q in range(4):
            nc.sync.dma_start(
                w2_s_raw[32 * q : 32 * q + 4, :, :].bitcast(I32),
                w2_scales[:, 4 * q : 4 * q + 4, :].rearrange("a r c -> r a c").bitcast(I32),
            )
        rest_t = first.tile([P, PACK], F32, name="rest_t", align_bytes=64, offset=6144)
        nc.sync.dma_start(rest_t[:], rest.rearrange("(p t) -> p t", t=PACK))
        ratio_t = first.tile([P, PACK], F32, name="ratio_t", align_bytes=64, offset=6144 + 64)
        nc.sync.dma_start(ratio_t[:], ratio.rearrange("(p t) -> p t", t=PACK))
        neg_rest = keep.tile([P, PACK], F32, name="neg_rest")
        nc.gpsimd.tensor_scalar(neg_rest[:], rest_t[:], -1.0, 0.0, ALU.mult, ALU.add)

        h_w = {(b, h): keep.tile([P, HALF], U32, name="h_w%d%d" % (b, h), align_bytes=64) for b in range(R_PASSES) for h in range(2)}
        h_s = {(b, h): keep.tile([P, HALF], U8, name="h_s%d%d" % (b, h), align_bytes=64) for b in range(R_PASSES) for h in range(2)}
        g2 = [keep.tile([P, S], F32, name="g2_%d" % t) for t in range(PACK)]

        steps = []
        order = ((0, 0), (0, 1), (1, 0), (2, 0), (1, 1), (2, 1))
        for b, h in order:
            widths = (128, 128, 128, 128) if (b, h) == order[-1] else (256, 256)
            c0 = 0
            for width in widths:
                steps.append((b, h, c0, width))
                c0 = c0 + width

        squares, roots, rounded = {}, {}, {}

        def square(i):
            b, h, c0, width = steps[i]
            squares[i] = ring.tile([P, width, PACK], F32, name="sq", bufs=3)
            for c in range(0, width, CHUNK):
                bank = psum.tile([P, PACK, CHUNK], F32, name="sway", tag="bank")
                scols = slice(h * HALF + c0 + c, h * HALF + c0 + c + CHUNK)
                for a in range(K_PASSES):
                    for t in range(PACK):
                        tc_ = slice(t * P, (t + 1) * P)
                        nc.tensor.matmul_mx(
                            bank[:, t, :],
                            lhsT=w1_w[b, a][:, tc_].bitcast(E4M3),
                            lhsT_scale=w1_s[b, a][:, tc_],
                            rhs=v_w[a][:, scols].bitcast(E4M3),
                            rhs_scale=v_s[4 * a : P, scols],
                            start=(a == 0 and t == 0),
                            stop=(a == K_PASSES - 1 and t == PACK - 1),
                        )
                nc.scalar.activation(squares[i][:, c : c + CHUNK, :], bank[:].rearrange("p t n -> p n t"), ACT.Square)

        def root(i):
            b, h, c0, width = steps[i]
            if c0 == 0:
                roots[b, h] = ring.tile([P, HALF, PACK], F32, name="root", bufs=5)
            nc.scalar.activation(roots[b, h][:, c0 : c0 + width, :], squares[i][:], ACT.Sqrt, bias=one[:])

        def piece(i):
            b, h, c0, width = steps[i]
            if (b, h) in order[-2:]:
                return slice(c0, c0 + width)
            return slice(0, HALF) if c0 + width == HALF else None

        def apply_gain(i):
            b, h = steps[i][:2]
            cols = piece(i)
            if cols is not None:
                width = cols.stop - cols.start
                rounded[i] = ring.tile([P, width, PACK], BF16, name="h_bf", align_bytes=64)
                nc.vector.tensor_tensor(
                    rounded[i][:], roots[b, h][:, cols, :], gain_t[:, b : b + 1, :].broadcast_to([P, width, PACK]), ALU.mult
                )

        def quantize_h(i):
            b, h = steps[i][:2]
            cols = piece(i)
            if cols is not None:
                nc.vector.quantize_mx(
                    h_w[b, h][:, cols].bitcast(E4M3), h_s[b, h][:, cols], rounded[i][:].rearrange("p n t -> p (n t)")
                )

        def deal_w2():
            w2_w = ring.tile([P, R_PASSES, 2 * N], U8, name="w2_w", tag="grouped", bufs=2, align_bytes=64)
            nc.vector.tensor_copy(
                w2_w[:].bitcast(U16).rearrange("p a (t q) -> p t a q", t=PACK),
                w2_raw[:].bitcast(U16).rearrange("p a (q t) -> p t a q", t=PACK),
            )
            w2_s = ring.tile([P, R_PASSES, N], U8, name="w2_s", tag="grouped", bufs=2, align_bytes=64)
            nc.vector.tensor_copy(
                w2_s[:].rearrange("p a (t q) -> p t a q", t=PACK),
                w2_s_raw[:].rearrange("p a (q t) -> p t a q", t=PACK),
            )
            return w2_w, w2_s

        banks = {}
        w2 = []

        def second(t, b, h, c0, width):
            cols = slice(c0, c0 + width)
            if b == 0:
                banks[h, t] = psum.tile([P, HALF], F32, name="feat", tag="bank")
            nc.tensor.matmul_mx(
                banks[h, t][:, cols],
                lhsT=w2[0][:, b, 2 * t * P : 2 * (t + 1) * P].bitcast(E2M1),
                lhsT_scale=w2[1][:, b, t * P : (t + 1) * P],
                rhs=h_w[b, h][:, cols].bitcast(E4M3),
                rhs_scale=h_s[b, h][:, cols],
                start=(b == 0),
                stop=(b == R_PASSES - 1 and c0 + width == HALF),
            )

        def first_half_features(t):
            for b in range(R_PASSES):
                second(t, b, 0, 0, HALF)
            if t != 1:
                nc.vector.tensor_scalar(g2[t][:, 0:HALF], banks[0, t][:], rest_t[:, t : t + 1], None, ALU.subtract)
            else:
                nc.scalar.activation(g2[t][:, 0:HALF], banks[0, t][:], ACT.Identity, bias=neg_rest[:, t : t + 1])

        n_steps = len(steps)
        for i in range(n_steps + 2):
            if i < n_steps:
                square(i)
            if 1 <= i <= n_steps:
                root(i - 1)
            if i < len(later):
                b, a = later[i]
                grouped = new_grouped()
                round_w1(grouped, raws[b, a], "vector")
            if 1 <= i <= n_steps:
                apply_gain(i - 1)
            if i < len(later):
                quantize_w1(b, a, grouped)
            if i == len(later):
                w2.extend(deal_w2())
            if i >= 2:
                quantize_h(i - 2)
            if i in (10, 11):
                first_half_features(2 * (i - 10))
                first_half_features(2 * (i - 10) + 1)
            if i in (12, 13):
                for t in range(PACK):
                    second(t, i - 12, 1, 0, HALF)
            for j in {13: (10, 11), 14: (12,), 15: (13,)}.get(i, ()):
                b, h, c0, width = steps[j]
                for t in range(PACK):
                    second(t, b, h, c0, width)

        for t in range(PACK):
            nc.scalar.activation(g2[t][:, HALF:S], banks[1, t][:], ACT.Identity, bias=neg_rest[:, t : t + 1])

        y_w = keep.tile([P, PAIRS], U32, name="y_w", align_bytes=64)
        y_s = keep.tile([P, PAIRS], U8, name="y_s", align_bytes=64)
        part = PAIRS // 2
        y_rows = out_0.rearrange("(p t) m -> p t m", t=PACK)
        words_out = out_1[0].rearrange("p m i -> p (m i)").bitcast(I32)
        y = keep.tile([P, PACK, PAIRS], F32, name="y")
        y_bf = keep.tile([P, PAIRS * PACK], BF16, name="y_bf", align_bytes=64)
        halves = (slice(0, part), slice(part, PAIRS))
        picks = [(t, slice(0, PAIRS)) for t in range(PACK - 1)] + [(PACK - 1, cols) for cols in halves]
        jibs, hooks = {}, {}

        def pick(i):
            t, cols = picks[i]
            lcols = slice(cols.start // 16, cols.stop // 16)
            jibs[i] = ring.tile([P, cols.stop - cols.start], F32, name="jib")
            nc.vector.tensor_copy(jibs[i][:], g2[t][:].indirect(pos1_t[:, lcols]))
            hooks[i] = ring.tile([P, cols.stop - cols.start], F32, name="hook")
            nc.vector.tensor_copy(hooks[i][:], g2[t][:].indirect(pos2_t[:, lcols]))

        def larger(i):
            t, cols = picks[i]
            nc.vector.scalar_tensor_tensor(y[:, t, cols], hooks[i][:], ratio_t[:, t : t + 1], jibs[i][:], ALU.mult, ALU.max)
            nc.sync.dma_start(y_rows[:, t, cols], y[:, t, cols])

        def round_y(copy, t0, cols):
            groups = slice(cols.start // 4, cols.stop // 4)
            dst = y_bf[:].rearrange("p (c i t) -> p c t i", i=4, t=PACK)[:, groups, t0 : t0 + 2, :]
            src = y[:].rearrange("p t (c i) -> p c t i", i=4)[:, groups, t0 : t0 + 2, :]
            copy(dst, src)

        def quantize_y(cols):
            nc.vector.quantize_mx(y_w[:, cols].bitcast(E4M3), y_s[:, cols], y_bf[:, PACK * cols.start : PACK * cols.stop])
            nc.scalar.dma_start(words_out[:, cols], y_w[:, cols].bitcast(I32))

        pick(0)
        for i in range(1, len(picks)):
            pick(i)
            larger(i - 1)
            if i == 2:
                round_y(nc.scalar.copy, 0, slice(0, PAIRS))
        round_y(nc.scalar.copy, 2, halves[0])
        larger(len(picks) - 1)
        quantize_y(halves[0])
        round_y(nc.vector.tensor_copy, 2, halves[1])
        quantize_y(halves[1])
        for q in range(4):
            queue = nc.sync if q < 3 else nc.scalar
            queue.dma_start(out_2[0, 4 * q : 4 * q + 4, :].bitcast(I32), y_s[32 * q : 32 * q + 4, :].bitcast(I32))
